import numpy as np
import ml_dtypes


def mxq(x, axis, fmt="e4m3"):
    dtype, down = {"e4m3": (ml_dtypes.float8_e4m3fn, 7), "e5m2": (ml_dtypes.float8_e5m2, 14)}[fmt]
    v = np.moveaxis(np.asarray(x, np.float32).astype(ml_dtypes.bfloat16).astype(np.float64), axis, -1)
    blocks = v.reshape(v.shape[:-1] + (-1, 32))
    amax = np.abs(blocks).max(-1, keepdims=True)
    byte = np.maximum(np.where(amax > 0, np.frexp(amax)[1] - 1 + 127, 0) - down, 1)
    scale = np.exp2(byte - 127.0)
    codes = (blocks / scale).astype(np.float32).astype(dtype).astype(np.float64)
    return np.moveaxis((codes * scale).reshape(v.shape), -1, axis)


WIDE = False


def mx_kscale(k):
    if not WIDE:
        return np.ones(k)
    levels = np.array([10, -10, 5, -5, 0])
    if k % 512:
        return np.exp2(np.random.permutation(np.resize(levels, k // 32))).repeat(32)
    a = np.empty((k // 512, 16))
    for p in range(k // 512):
        a[p, :8] = np.random.permutation(np.resize(levels, 8))
        for g in range(8):
            far = levels[np.abs(levels - a[p, g]) >= 10]
            a[p, g + 8] = far[np.random.randint(len(far))]
    return np.exp2(a.ravel()).repeat(32)


def f64(x):
    return np.asarray(x).astype(np.float64)


def striped(idx):
    return np.tile(idx.reshape(-1, 16).T, (8, 1)).astype(np.uint16)


def unstriped(offs):
    return offs[:16].T.reshape(-1).astype(np.int64)


def pack_weight(w):
    k, n = w.shape
    w = f64(np.asarray(w, np.float32).astype(ml_dtypes.bfloat16)).reshape(k // 32, 32, n)
    amax = np.abs(w).max(1)
    byte = np.clip(np.where(amax > 0, np.frexp(amax)[1] - 1 + 127 - 7, 1), 1, 254)
    scaled = (w * np.exp2(127.0 - byte)[:, None, :]).reshape(k, n).astype(np.float32)
    words = np.ascontiguousarray(scaled.reshape(k // 512, 128, 4, n).transpose(0, 1, 3, 2)).astype(ml_dtypes.float8_e4m3fn).view(np.uint8)
    return words, np.ascontiguousarray(byte.astype(np.uint8).reshape(k // 512, 16, n))


def unpack_weight(words, scales):
    g, p, n, _ = words.shape
    vals = np.ascontiguousarray(words).view(ml_dtypes.float8_e4m3fn).astype(np.float64) * np.repeat(np.exp2(scales.astype(np.float64) - 127.0), 8, axis=1)[..., None]
    return vals.transpose(0, 1, 3, 2).reshape(g * 512, n)


def planes(y):
    n, m = y.shape
    v = y.astype(np.float32).astype(ml_dtypes.bfloat16).astype(np.float64).reshape(n // 32, 32, m)
    top = np.abs(v).max(1)
    byte = np.clip(np.where(top > 0, np.frexp(top)[1] - 1 + 127 - 7, 1), 1, 254)
    codes = (v * np.exp2(127.0 - byte)[:, None, :]).reshape(n, m).astype(np.float32).astype(ml_dtypes.float8_e4m3fn).view(np.uint8)
    words = codes.reshape(n // 512, 128, 4, m).transpose(0, 1, 3, 2)
    return np.ascontiguousarray(words), np.ascontiguousarray(byte.astype(np.uint8).reshape(n // 512, 16, m))


def gelu(v):
    return 0.5 * v * (1.0 + np.tanh(np.sqrt(2.0 / np.pi) * (v + 0.044715 * v**3)))


K, T, S, J, H, N, W = 1024, 1024, 512, 512, 512, 512, 2048


def setup_inputs():
    n = np.random.standard_normal
    s = mx_kscale(K)[:, None]
    u = mx_kscale(H)
    r = mx_kscale(J)[:, None]
    packed_xT = pack_weight(n((K, T)) * s)
    packed_eT = pack_weight(n((J, W)) * r)
    packed_w3 = pack_weight(n((H, N)) / np.sqrt(H) / u[:, None])
    return {
        "x_words": packed_xT[0],
        "x_scales": packed_xT[1],
        "e_words": packed_eT[0],
        "e_scales": packed_eT[1],
        "w1": (n((K, H)) / np.sqrt(2 * K) / s * u).astype(np.float32),
        "w2": (n((J, H)) / np.sqrt(2 * J) / r * u).astype(np.float32),
        "w3_words": packed_w3[0],
        "w3_scales": packed_w3[1],
        "bias": (0.3 * n((H, 1)) * u[:, None]).astype(np.float32),
        "offs": striped(np.random.permutation(T)[:S]),
        "item": striped(np.random.permutation(W)[:S]),
    }


def reference(x_words, x_scales, e_words, e_scales, w1, w2, w3_words, w3_scales, bias, offs, item):
    xq = unpack_weight(x_words, x_scales)[:, unstriped(offs)]
    e_item = unpack_weight(e_words, e_scales)[:, unstriped(item)]
    h = gelu((mxq(f64(w1), 0, "e4m3").T @ xq + mxq(f64(w2), 0, "e4m3").T @ e_item) + f64(bias))
    out_0 = unpack_weight(w3_words, w3_scales).T @ mxq(h, 0, "e4m3")
    return (out_0,) + planes(out_0)

@@ -1,0 +1,205 @@
+from contextlib import ExitStack
+
+import concourse.mybir as mybir
+
+F32 = mybir.dt.float32
+BF16 = mybir.dt.bfloat16
+I32 = mybir.dt.int32
+U32 = mybir.dt.uint32
+U16 = mybir.dt.uint16
+U8 = mybir.dt.uint8
+FP8X4 = mybir.dt.float8_e4m3fn_x4
+GELU = mybir.ActivationFunctionType.Gelu_apprx_tanh
+
+P = 128
+PACK = 4
+K_PASS = P * PACK
+T, W, S, H, N = 1024, 2048, 512, 512, 512
+CHUNK = 128
+CHUNKS = S // CHUNK
+FLOPS = 2 * 512 * 512 * (1024 + 512 + 512)
+
+
+def tile_picked_zuit_gelu_po_kernel(
+    tc, x_words, x_scales, e_words, e_scales, w1, w2, w3_words, w3_scales, bias, offs, item, out_0, out_1, out_2
+):
+    nc = tc.nc
+    with ExitStack() as ctx:
+        keep = ctx.enter_context(tc.tile_pool(name="keep", bufs=1))
+        psum = ctx.enter_context(tc.psum_pool(name="psum", bufs=1))
+
+        def sb(shape, dtype, name, tag=None):
+            return keep.tile(shape, dtype, name=name, tag=tag or name, align_bytes=64)
+
+        offs_t = keep.tile([P, S // 16], U16, name="offs_t")
+        item_t = keep.tile([P, S // 16], U16, name="item_t")
+        bias_t = sb([P, PACK], F32, "bias_t")
+        xw = [sb([P, T], I32, f"xw{g}") for g in range(2)]
+        ew = sb([P, W], I32, "ew")
+        xs = sb([P, T], U8, "xs")
+        es = sb([P, W], U8, "es", "shared")
+        w3s = sb([P, N], U8, "w3s")
+        w3w = sb([P, N], I32, "w3w")
+        raw = [sb([P, PACK, H], F32, f"raw{g}") for g in range(3)]
+        rows = [w1[0:K_PASS, :], w1[K_PASS : 2 * K_PASS, :], w2]
+
+        nc.vector.memset(xs[:].bitcast(I32), 0)
+        nc.vector.memset(es[:].bitcast(I32), 0)
+        nc.gpsimd.memset(w3s[:].bitcast(I32), 0)
+
+        def load_weight(g, lo, hi):
+            view = rows[g].rearrange("(p j) c -> p j c", j=PACK)
+            nc.sync.dma_start(out=raw[g][:, lo:hi, :], in_=view[:, lo:hi, :])
+
+        def load_words(dst, src):
+            nc.sync.dma_start(out=dst, in_=src.rearrange("p n t -> p (n t)").bitcast(I32))
+
+        def load_scales(queue, dst, src, first_row):
+            passes = src.shape[0]
+            for q in range(4):
+                lo = 32 * q + first_row
+                queue.dma_start(
+                    out=dst[lo : lo + 4 * passes, :].bitcast(I32), in_=src[:, 4 * q : 4 * q + 4, :].bitcast(I32)
+                )
+
+        load_scales(nc.gpsimd, w3s, w3_scales, 12)
+        load_weight(0, 0, 4)
+        nc.sync.dma_start(offs_t[:], offs)
+        load_scales(nc.sync, xs, x_scales, 0)
+        load_weight(1, 0, 4)
+        nc.sync.dma_start(item_t[:], item)
+        load_scales(nc.sync, es, e_scales, 8)
+        load_weight(2, 0, 4)
+        nc.sync.dma_start(out=bias_t[:], in_=bias.rearrange("(p t) o -> p (t o)", t=PACK))
+        load_words(xw[0][:], x_words[0])
+        load_words(ew[:], e_words[0])
+        load_words(xw[1][:], x_words[1])
+        load_words(w3w[:], w3_words[0])
+
+        wq = [sb([P, H], U32, "wq0"), None, sb([P, H], U32, "wq2")]
+        wsc = [sb([P, H], U8, f"wsc{g}") for g in range(3)]
+        wb = [sb([P, H * PACK], BF16, f"wb{g}") for g in range(3)]
+
+        def round_weight(g):
+            nc.scalar.copy(
+                out=wb[g][:].rearrange("p (t m j) -> p m j t", t=PACK, j=PACK),
+                in_=raw[g][:].rearrange("p j (m t) -> p m j t", t=PACK),
+            )
+
+        def quant_weight(g):
+            nc.vector.quantize_mx(out=wq[g][:].bitcast(FP8X4), scales=wsc[g][:], in_=wb[g][:])
+
+        xsg = sb([P, S], U8, "xsg")
+        esg = sb([P, S], U8, "esg")
+        xg = [sb([P, S], U32, f"xg{g}") for g in range(2)]
+        eg = sb([P, S], U32, "eg")
+        w3sd = sb([P, N], U8, "w3sd")
+        w3wd = sb([P, N], I32, "w3wd")
+
+        def gather_words(dst, table, lst, lo, hi):
+            nc.vector.tensor_copy(out=dst[:, lo:hi], in_=table[:].bitcast(U32).indirect(lst[:, lo // 16 : hi // 16]))
+
+        hbank = [psum.tile([P, PACK, CHUNK], F32, name=f"hbank{c}") for c in range(CHUNKS)]
+        obank = [psum.tile([P, PACK, CHUNK], F32, name=f"obank{c}") for c in range(CHUNKS)]
+
+        def first_layer(g, codes, plane, c, first, last):
+            cols = slice(c * CHUNK, (c + 1) * CHUNK)
+            for t in range(PACK):
+                m = slice(t * P, (t + 1) * P)
+                nc.tensor.matmul_mx(
+                    out=hbank[c][:, t, :],
+                    lhsT=wq[g][:, m].bitcast(FP8X4),
+                    lhsT_scale=wsc[g][:, m],
+                    rhs=codes[:, cols].bitcast(FP8X4),
+                    rhs_scale=plane[:, cols],
+                    start=first and t == 0,
+                    stop=last and t == PACK - 1,
+                )
+
+        round_weight(0)
+        nc.gpsimd.tensor_copy(
+            out=w3sd[:].rearrange("p (t m) -> p t m", t=PACK), in_=w3s[:].rearrange("p (m t) -> p t m", t=PACK)
+        )
+        nc.gpsimd.tensor_copy(
+            out=w3wd[:].rearrange("p (t m) -> p m t", t=PACK), in_=w3w[:].rearrange("p (m t) -> p m t", t=PACK)
+        )
+        nc.vector.tensor_copy(out=xsg[:], in_=xs[:].indirect(offs_t[:]))
+        round_weight(1)
+        quant_weight(0)
+        nc.vector.tensor_copy(out=esg[:], in_=es[:].indirect(item_t[:]))
+        round_weight(2)
+        wq[1] = sb([P, H], U32, "wq1", "shared")
+        quant_weight(1)
+        for half in range(2):
+            gather_words(xg[0], xw[0], offs_t, half * 256, (half + 1) * 256)
+            for c in (2 * half, 2 * half + 1):
+                first_layer(0, xg[0], xsg[0:P, :], c, True, False)
+        quant_weight(2)
+        for half in range(2):
+            gather_words(eg, ew, item_t, half * 256, (half + 1) * 256)
+            for c in (2 * half, 2 * half + 1):
+                first_layer(2, eg, esg[8:P, :], c, False, False)
+        for c in range(CHUNKS):
+            gather_words(xg[1], xw[1], offs_t, c * CHUNK, (c + 1) * CHUNK)
+            first_layer(1, xg[1], xsg[4:P, :], c, False, True)
+
+        hb = [sb([P, PACK, CHUNK], BF16, f"hb{c}") for c in range(CHUNKS)]
+        hi4 = [sb([P, CHUNK * PACK], BF16, f"hi4{c}") for c in range(CHUNKS)]
+        hq = [sb([P, CHUNK], U32, f"hq{c}") for c in range(CHUNKS)]
+        hs = [sb([P, CHUNK], U8, f"hs{c}") for c in range(CHUNKS)]
+        y = [sb([P, PACK, CHUNK], F32, f"y{c}") for c in range(CHUNKS)]
+        yb = [sb([P, CHUNK * PACK], BF16, f"yb{c}") for c in range(CHUNKS)]
+        yq = sb([P, S], I32, "yq")
+        ys = sb([P, S], U8, "ys")
+        out_rows = out_0.rearrange("(p t) j -> p t j", t=PACK)
+        out_words = out_1[0].rearrange("p n t -> p (n t)").bitcast(I32)
+
+        def interleave(dst, src):
+            nc.vector.tensor_copy(
+                out=dst[:].rearrange("p (c i t) -> p c t i", i=4, t=PACK),
+                in_=src[:].rearrange("p t (c i) -> p c t i", i=4),
+            )
+
+        def act(c):
+            for t in range(PACK):
+                nc.scalar.activation(out=hb[c][:, t, :], in_=hbank[c][:, t, :], func=GELU, bias=bias_t[:, t : t + 1])
+
+        def second(c):
+            nc.vector.quantize_mx(out=hq[c][:].bitcast(FP8X4), scales=hs[c][:], in_=hi4[c][:])
+            for t in range(PACK):
+                m = slice(t * P, (t + 1) * P)
+                nc.tensor.matmul_mx(
+                    out=obank[c][:, t, :],
+                    lhsT=w3wd[:, m].bitcast(FP8X4),
+                    lhsT_scale=w3sd[12:P, m],
+                    rhs=hq[c][:].bitcast(FP8X4),
+                    rhs_scale=hs[c][:],
+                    start=True,
+                    stop=True,
+                )
+
+        def leave(c):
+            cols = slice(c * CHUNK, (c + 1) * CHUNK)
+            nc.scalar.copy(out=y[c][:], in_=obank[c][:])
+            nc.sync.dma_start(out=out_rows[:, :, cols], in_=y[c][:])
+            interleave(yb[c], y[c])
+
+        def planes(c):
+            cols = slice(c * CHUNK, (c + 1) * CHUNK)
+            nc.vector.quantize_mx(out=yq[:, cols].bitcast(FP8X4), scales=ys[:, cols], in_=yb[c][:])
+
+        for c in range(CHUNKS):
+            act(c)
+            interleave(hi4[c], hb[c])
+            second(c)
+        for c in range(CHUNKS):
+            leave(c)
+            planes(c)
+            if c == CHUNKS - 2:
+                nc.sync.dma_start(out=out_words[:, : S - CHUNK], in_=yq[:, : S - CHUNK])
+        nc.sync.dma_start(out=out_words[:, S - CHUNK :], in_=yq[:, S - CHUNK :])
+        for q in range(4):
+            queue = nc.scalar if q % 2 == 0 else nc.sync
+            queue.dma_start(
+                out=out_2[0, 4 * q : 4 * q + 4, :].bitcast(I32), in_=ys[32 * q : 32 * q + 4, :].bitcast(I32)
+            )

@@ -34,27 +34,22 @@ def tile_picked_zuit_gelu_po_kernel(
         offs_t = keep.tile([P, S // 16], U16, name="offs_t")
         item_t = keep.tile([P, S // 16], U16, name="item_t")
         bias_t = sb([P, PACK], F32, "bias_t")
-        xw = [sb([P, T], I32, f"xw{g}") for g in range(2)]
+        xw = [sb([P, T], I32, "xw0", "shared1"), sb([P, T], I32, "xw1")]
         ew = sb([P, W], I32, "ew")
-        xs = sb([P, T], U8, "xs")
-        es = sb([P, W], U8, "es", "shared")
+        xs = sb([P, T], U8, "xs", "shared")
+        es = sb([P, W], U8, "es")
         w3s = sb([P, N], U8, "w3s")
         w3w = sb([P, N], I32, "w3w")
         raw = [sb([P, PACK, H], F32, f"raw{g}") for g in range(3)]
         rows = [w1[0:K_PASS, :], w1[K_PASS : 2 * K_PASS, :], w2]
 
-        nc.vector.memset(xs[:].bitcast(I32), 0)
-        nc.vector.memset(es[:].bitcast(I32), 0)
-        nc.gpsimd.memset(w3s[:].bitcast(I32), 0)
-
-        def load_weight(g, lo, hi):
-            view = rows[g].rearrange("(p j) c -> p j c", j=PACK)
-            nc.sync.dma_start(out=raw[g][:, lo:hi, :], in_=view[:, lo:hi, :])
+        def load_weight(g):
+            nc.sync.dma_start(out=raw[g][:], in_=rows[g].rearrange("(p j) c -> p j c", j=PACK))
 
         def load_words(dst, src):
-            nc.sync.dma_start(out=dst, in_=src.rearrange("p n t -> p (n t)").bitcast(I32))
+            nc.sync.dma_start(out=dst[:], in_=src.rearrange("p n t -> p (n t)").bitcast(I32))
 
-        def load_scales(queue, dst, src, first_row):
+        def load_scales_by_quadrant(queue, dst, src, first_row):
             passes = src.shape[0]
             for q in range(4):
                 lo = 32 * q + first_row
@@ -62,21 +57,28 @@ def tile_picked_zuit_gelu_po_kernel(
                     out=dst[lo : lo + 4 * passes, :].bitcast(I32), in_=src[:, 4 * q : 4 * q + 4, :].bitcast(I32)
                 )
 
-        load_scales(nc.gpsimd, w3s, w3_scales, 12)
-        load_weight(0, 0, 4)
-        nc.sync.dma_start(offs_t[:], offs)
-        load_scales(nc.sync, xs, x_scales, 0)
-        load_weight(1, 0, 4)
-        nc.sync.dma_start(item_t[:], item)
-        load_scales(nc.sync, es, e_scales, 8)
-        load_weight(2, 0, 4)
-        nc.sync.dma_start(out=bias_t[:], in_=bias.rearrange("(p t) o -> p (t o)", t=PACK))
-        load_words(xw[0][:], x_words[0])
-        load_words(ew[:], e_words[0])
-        load_words(xw[1][:], x_words[1])
-        load_words(w3w[:], w3_words[0])
+        def load_scales_by_row(queue, dst, src, first_row):
+            for r in range(4):
+                queue.dma_start(out=dst[first_row + r : P : 32, :].bitcast(I32), in_=src[0, r:16:4, :].bitcast(I32))
 
-        wq = [sb([P, H], U32, "wq0"), None, sb([P, H], U32, "wq2")]
+        nc.vector.memset(xs[:].bitcast(I32), 0)
+        nc.vector.memset(es[:].bitcast(I32), 0)
+        nc.gpsimd.memset(w3s[:].bitcast(I32), 0)
+        load_scales_by_row(nc.gpsimd, w3s, w3_scales, 12)
+        load_weight(0)
+        nc.sync.dma_start(offs_t[:], offs)
+        load_scales_by_quadrant(nc.sync, xs, x_scales, 0)
+        load_weight(1)
+        nc.sync.dma_start(item_t[:], item)
+        load_scales_by_row(nc.sync, es, e_scales, 8)
+        load_words(xw[0], x_words[0])
+        load_weight(2)
+        nc.sync.dma_start(out=bias_t[:], in_=bias.rearrange("(p t) o -> p (t o)", t=PACK))
+        load_words(xw[1], x_words[1])
+        load_words(ew, e_words[0])
+        load_words(w3w, w3_words[0])
+
+        wq = [None, None, sb([P, H], U32, "wq2")]
         wsc = [sb([P, H], U8, f"wsc{g}") for g in range(3)]
         wb = [sb([P, H * PACK], BF16, f"wb{g}") for g in range(3)]
 
@@ -94,7 +96,7 @@ def tile_picked_zuit_gelu_po_kernel(
         xg = [sb([P, S], U32, f"xg{g}") for g in range(2)]
         eg = sb([P, S], U32, "eg")
         w3sd = sb([P, N], U8, "w3sd")
-        w3wd = sb([P, N], I32, "w3wd")
+        w3wd = sb([P, N], U32, "w3wd")
 
         def gather_words(dst, table, lst, lo, hi):
             nc.vector.tensor_copy(out=dst[:, lo:hi], in_=table[:].bitcast(U32).indirect(lst[:, lo // 16 : hi // 16]))
@@ -116,32 +118,32 @@ def tile_picked_zuit_gelu_po_kernel(
                     stop=last and t == PACK - 1,
                 )
 
-        round_weight(0)
         nc.gpsimd.tensor_copy(
             out=w3sd[:].rearrange("p (t m) -> p t m", t=PACK), in_=w3s[:].rearrange("p (m t) -> p t m", t=PACK)
         )
-        nc.gpsimd.tensor_copy(
-            out=w3wd[:].rearrange("p (t m) -> p m t", t=PACK), in_=w3w[:].rearrange("p (m t) -> p m t", t=PACK)
-        )
+        round_weight(0)
         nc.vector.tensor_copy(out=xsg[:], in_=xs[:].indirect(offs_t[:]))
         round_weight(1)
+        wq[0] = sb([P, H], U32, "wq0", "shared")
         quant_weight(0)
         nc.vector.tensor_copy(out=esg[:], in_=es[:].indirect(item_t[:]))
         round_weight(2)
-        wq[1] = sb([P, H], U32, "wq1", "shared")
-        quant_weight(1)
-        for half in range(2):
-            gather_words(xg[0], xw[0], offs_t, half * 256, (half + 1) * 256)
-            for c in (2 * half, 2 * half + 1):
-                first_layer(0, xg[0], xsg[0:P, :], c, True, False)
+        for g in range(2):
+            if g == 1:
+                wq[1] = sb([P, H], U32, "wq1", "shared1")
+                quant_weight(1)
+            for half in range(2):
+                gather_words(xg[g], xw[g], offs_t, half * 256, (half + 1) * 256)
+                for c in (2 * half, 2 * half + 1):
+                    first_layer(g, xg[g], xsg[4 * g : P, :], c, g == 0, False)
         quant_weight(2)
-        for half in range(2):
-            gather_words(eg, ew, item_t, half * 256, (half + 1) * 256)
-            for c in (2 * half, 2 * half + 1):
-                first_layer(2, eg, esg[8:P, :], c, False, False)
         for c in range(CHUNKS):
-            gather_words(xg[1], xw[1], offs_t, c * CHUNK, (c + 1) * CHUNK)
-            first_layer(1, xg[1], xsg[4:P, :], c, False, True)
+            gather_words(eg, ew, item_t, c * CHUNK, (c + 1) * CHUNK)
+            first_layer(2, eg, esg[8:P, :], c, False, True)
+        nc.vector.tensor_copy(
+            out=w3wd[:].bitcast(I32).rearrange("p (t m) -> p m t", t=PACK),
+            in_=w3w[:].rearrange("p (m t) -> p m t", t=PACK),
+        )
 
         hb = [sb([P, PACK, CHUNK], BF16, f"hb{c}") for c in range(CHUNKS)]
         hi4 = [sb([P, CHUNK * PACK], BF16, f"hi4{c}") for c in range(CHUNKS)]
@@ -165,6 +167,7 @@ def tile_picked_zuit_gelu_po_kernel(
                 nc.scalar.activation(out=hb[c][:, t, :], in_=hbank[c][:, t, :], func=GELU, bias=bias_t[:, t : t + 1])
 
         def second(c):
+            interleave(hi4[c], hb[c])
             nc.vector.quantize_mx(out=hq[c][:].bitcast(FP8X4), scales=hs[c][:], in_=hi4[c][:])
             for t in range(PACK):
                 m = slice(t * P, (t + 1) * P)
@@ -178,26 +181,30 @@ def tile_picked_zuit_gelu_po_kernel(
                     stop=True,
                 )
 
-        def leave(c):
-            cols = slice(c * CHUNK, (c + 1) * CHUNK)
-            nc.scalar.copy(out=y[c][:], in_=obank[c][:])
-            nc.sync.dma_start(out=out_rows[:, :, cols], in_=y[c][:])
-            interleave(yb[c], y[c])
+        def leave(c, copy):
+            copy(out=y[c][:], in_=obank[c][:])
+            nc.sync.dma_start(out=out_rows[:, :, c * CHUNK : (c + 1) * CHUNK], in_=y[c][:])
+
+        def round_from_psum(c):
+            nc.scalar.copy(out=yb[c][:].rearrange("p (n t) -> p n t", t=PACK), in_=obank[c][:].rearrange("p t n -> p n t"))
 
         def planes(c):
             cols = slice(c * CHUNK, (c + 1) * CHUNK)
             nc.vector.quantize_mx(out=yq[:, cols].bitcast(FP8X4), scales=ys[:, cols], in_=yb[c][:])
 
+        def store_words(lo, hi):
+            nc.sync.dma_start(out=out_words[:, lo * CHUNK : hi * CHUNK], in_=yq[:, lo * CHUNK : hi * CHUNK])
+
         for c in range(CHUNKS):
             act(c)
-            interleave(hi4[c], hb[c])
             second(c)
         for c in range(CHUNKS):
-            leave(c)
+            leave(c, nc.scalar.copy)
+            interleave(yb[c], y[c])
             planes(c)
             if c == CHUNKS - 2:
-                nc.sync.dma_start(out=out_words[:, : S - CHUNK], in_=yq[:, : S - CHUNK])
-        nc.sync.dma_start(out=out_words[:, S - CHUNK :], in_=yq[:, S - CHUNK :])
+                store_words(0, 3)
+        store_words(3, 4)
         for q in range(4):
             queue = nc.scalar if q % 2 == 0 else nc.sync
             queue.dma_start(

from contextlib import ExitStack

import concourse.mybir as mybir

F32 = mybir.dt.float32
BF16 = mybir.dt.bfloat16
I32 = mybir.dt.int32
U32 = mybir.dt.uint32
U16 = mybir.dt.uint16
U8 = mybir.dt.uint8
FP8X4 = mybir.dt.float8_e4m3fn_x4
GELU = mybir.ActivationFunctionType.Gelu_apprx_tanh

P = 128
PACK = 4
K_PASS = P * PACK
T, W, S, H, N = 1024, 2048, 512, 512, 512
CHUNK = 128
CHUNKS = S // CHUNK
FLOPS = 2 * 512 * 512 * (1024 + 512 + 512)


def tile_picked_zuit_gelu_po_kernel(
    tc, x_words, x_scales, e_words, e_scales, w1, w2, w3_words, w3_scales, bias, offs, item, out_0, out_1, out_2
):
    nc = tc.nc
    with ExitStack() as ctx:
        keep = ctx.enter_context(tc.tile_pool(name="keep", bufs=1))
        psum = ctx.enter_context(tc.psum_pool(name="psum", bufs=1))

        def sb(shape, dtype, name, tag=None):
            return keep.tile(shape, dtype, name=name, tag=tag or name, align_bytes=64)

        offs_t = keep.tile([P, S // 16], U16, name="offs_t")
        item_t = keep.tile([P, S // 16], U16, name="item_t")
        bias_t = sb([P, PACK], F32, "bias_t")
        xw = [sb([P, T], I32, "xw0", "shared1"), sb([P, T], I32, "xw1")]
        ew = sb([P, W], I32, "ew")
        xs = sb([P, T], U8, "xs", "shared")
        es = sb([P, W], U8, "es")
        w3s = sb([P, N], U8, "w3s")
        w3w = sb([P, N], I32, "w3w")
        raw = [sb([P, PACK, H], F32, f"raw{g}") for g in range(3)]
        rows = [w1[0:K_PASS, :], w1[K_PASS : 2 * K_PASS, :], w2]

        def load_weight(g):
            nc.sync.dma_start(out=raw[g][:], in_=rows[g].rearrange("(p j) c -> p j c", j=PACK))

        def load_words(dst, src):
            nc.sync.dma_start(out=dst[:], in_=src.rearrange("p n t -> p (n t)").bitcast(I32))

        def load_scales_by_quadrant(queue, dst, src, first_row):
            passes = src.shape[0]
            for q in range(4):
                lo = 32 * q + first_row
                queue.dma_start(
                    out=dst[lo : lo + 4 * passes, :].bitcast(I32), in_=src[:, 4 * q : 4 * q + 4, :].bitcast(I32)
                )

        def load_scales_by_row(queue, dst, src, first_row):
            for r in range(4):
                queue.dma_start(out=dst[first_row + r : P : 32, :].bitcast(I32), in_=src[0, r:16:4, :].bitcast(I32))

        nc.vector.memset(xs[:].bitcast(I32), 0)
        nc.vector.memset(es[:].bitcast(I32), 0)
        nc.gpsimd.memset(w3s[:].bitcast(I32), 0)
        load_scales_by_row(nc.gpsimd, w3s, w3_scales, 12)
        load_weight(0)
        nc.sync.dma_start(offs_t[:], offs)
        load_scales_by_quadrant(nc.sync, xs, x_scales, 0)
        load_weight(1)
        nc.sync.dma_start(item_t[:], item)
        load_scales_by_row(nc.sync, es, e_scales, 8)
        load_words(xw[0], x_words[0])
        load_weight(2)
        nc.sync.dma_start(out=bias_t[:], in_=bias.rearrange("(p t) o -> p (t o)", t=PACK))
        load_words(xw[1], x_words[1])
        load_words(ew, e_words[0])
        load_words(w3w, w3_words[0])

        wq = [None, None, sb([P, H], U32, "wq2")]
        wsc = [sb([P, H], U8, f"wsc{g}") for g in range(3)]
        wb = [sb([P, H * PACK], BF16, f"wb{g}") for g in range(3)]

        def round_weight(g):
            nc.scalar.copy(
                out=wb[g][:].rearrange("p (t m j) -> p m j t", t=PACK, j=PACK),
                in_=raw[g][:].rearrange("p j (m t) -> p m j t", t=PACK),
            )

        def quant_weight(g):
            nc.vector.quantize_mx(out=wq[g][:].bitcast(FP8X4), scales=wsc[g][:], in_=wb[g][:])

        xsg = sb([P, S], U8, "xsg")
        esg = sb([P, S], U8, "esg")
        xg = [sb([P, S], U32, f"xg{g}") for g in range(2)]
        eg = sb([P, S], U32, "eg")
        w3sd = sb([P, N], U8, "w3sd")
        w3wd = sb([P, N], U32, "w3wd")

        def gather_words(dst, table, lst, lo, hi):
            nc.vector.tensor_copy(out=dst[:, lo:hi], in_=table[:].bitcast(U32).indirect(lst[:, lo // 16 : hi // 16]))

        hbank = [psum.tile([P, PACK, CHUNK], F32, name=f"hbank{c}") for c in range(CHUNKS)]
        obank = [psum.tile([P, PACK, CHUNK], F32, name=f"obank{c}") for c in range(CHUNKS)]

        def first_layer(g, codes, plane, c, first, last):
            cols = slice(c * CHUNK, (c + 1) * CHUNK)
            for t in range(PACK):
                m = slice(t * P, (t + 1) * P)
                nc.tensor.matmul_mx(
                    out=hbank[c][:, t, :],
                    lhsT=wq[g][:, m].bitcast(FP8X4),
                    lhsT_scale=wsc[g][:, m],
                    rhs=codes[:, cols].bitcast(FP8X4),
                    rhs_scale=plane[:, cols],
                    start=first and t == 0,
                    stop=last and t == PACK - 1,
                )

        nc.gpsimd.tensor_copy(
            out=w3sd[:].rearrange("p (t m) -> p t m", t=PACK), in_=w3s[:].rearrange("p (m t) -> p t m", t=PACK)
        )
        round_weight(0)
        nc.vector.tensor_copy(out=xsg[:], in_=xs[:].indirect(offs_t[:]))
        round_weight(1)
        wq[0] = sb([P, H], U32, "wq0", "shared")
        quant_weight(0)
        nc.vector.tensor_copy(out=esg[:], in_=es[:].indirect(item_t[:]))
        round_weight(2)
        for g in range(2):
            if g == 1:
                wq[1] = sb([P, H], U32, "wq1", "shared1")
                quant_weight(1)
            for half in range(2):
                gather_words(xg[g], xw[g], offs_t, half * 256, (half + 1) * 256)
                for c in (2 * half, 2 * half + 1):
                    first_layer(g, xg[g], xsg[4 * g : P, :], c, g == 0, False)
        quant_weight(2)
        for c in range(CHUNKS):
            gather_words(eg, ew, item_t, c * CHUNK, (c + 1) * CHUNK)
            first_layer(2, eg, esg[8:P, :], c, False, True)
        nc.vector.tensor_copy(
            out=w3wd[:].bitcast(I32).rearrange("p (t m) -> p m t", t=PACK),
            in_=w3w[:].rearrange("p (m t) -> p m t", t=PACK),
        )

        hb = [sb([P, PACK, CHUNK], BF16, f"hb{c}") for c in range(CHUNKS)]
        hi4 = [sb([P, CHUNK * PACK], BF16, f"hi4{c}") for c in range(CHUNKS)]
        hq = [sb([P, CHUNK], U32, f"hq{c}") for c in range(CHUNKS)]
        hs = [sb([P, CHUNK], U8, f"hs{c}") for c in range(CHUNKS)]
        y = [sb([P, PACK, CHUNK], F32, f"y{c}") for c in range(CHUNKS)]
        yb = [sb([P, CHUNK * PACK], BF16, f"yb{c}") for c in range(CHUNKS)]
        yq = sb([P, S], I32, "yq")
        ys = sb([P, S], U8, "ys")
        out_rows = out_0.rearrange("(p t) j -> p t j", t=PACK)
        out_words = out_1[0].rearrange("p n t -> p (n t)").bitcast(I32)

        def interleave(dst, src):
            nc.vector.tensor_copy(
                out=dst[:].rearrange("p (c i t) -> p c t i", i=4, t=PACK),
                in_=src[:].rearrange("p t (c i) -> p c t i", i=4),
            )

        def act(c):
            for t in range(PACK):
                nc.scalar.activation(out=hb[c][:, t, :], in_=hbank[c][:, t, :], func=GELU, bias=bias_t[:, t : t + 1])

        def second(c):
            interleave(hi4[c], hb[c])
            nc.vector.quantize_mx(out=hq[c][:].bitcast(FP8X4), scales=hs[c][:], in_=hi4[c][:])
            for t in range(PACK):
                m = slice(t * P, (t + 1) * P)
                nc.tensor.matmul_mx(
                    out=obank[c][:, t, :],
                    lhsT=w3wd[:, m].bitcast(FP8X4),
                    lhsT_scale=w3sd[12:P, m],
                    rhs=hq[c][:].bitcast(FP8X4),
                    rhs_scale=hs[c][:],
                    start=True,
                    stop=True,
                )

        def leave(c, copy):
            copy(out=y[c][:], in_=obank[c][:])
            nc.sync.dma_start(out=out_rows[:, :, c * CHUNK : (c + 1) * CHUNK], in_=y[c][:])

        def round_from_psum(c):
            nc.scalar.copy(out=yb[c][:].rearrange("p (n t) -> p n t", t=PACK), in_=obank[c][:].rearrange("p t n -> p n t"))

        def planes(c):
            cols = slice(c * CHUNK, (c + 1) * CHUNK)
            nc.vector.quantize_mx(out=yq[:, cols].bitcast(FP8X4), scales=ys[:, cols], in_=yb[c][:])

        def store_words(lo, hi):
            nc.sync.dma_start(out=out_words[:, lo * CHUNK : hi * CHUNK], in_=yq[:, lo * CHUNK : hi * CHUNK])

        for c in range(CHUNKS):
            act(c)
            second(c)
        for c in range(CHUNKS):
            leave(c, nc.scalar.copy)
            interleave(yb[c], y[c])
            planes(c)
            if c == CHUNKS - 2:
                store_words(0, 3)
        store_words(3, 4)
        for q in range(4):
            queue = nc.scalar if q % 2 == 0 else nc.sync
            queue.dma_start(
                out=out_2[0, 4 * q : 4 * q + 4, :].bitcast(I32), in_=ys[32 * q : 32 * q + 4, :].bitcast(I32)
            )
